import numpy as np
import ml_dtypes


def mxq(x, axis, fmt="e4m3"):
    dtype, down = {"e4m3": (ml_dtypes.float8_e4m3fn, 7), "e5m2": (ml_dtypes.float8_e5m2, 14)}[fmt]
    v = np.moveaxis(np.asarray(x, np.float32).astype(ml_dtypes.bfloat16).astype(np.float64), axis, -1)
    blocks = v.reshape(v.shape[:-1] + (-1, 32))
    amax = np.abs(blocks).max(-1, keepdims=True)
    byte = np.maximum(np.where(amax > 0, np.frexp(amax)[1] - 1 + 127, 0) - down, 1)
    scale = np.exp2(byte - 127.0)
    codes = (blocks / scale).astype(np.float32).astype(dtype).astype(np.float64)
    return np.moveaxis((codes * scale).reshape(v.shape), -1, axis)


WIDE = False


def mx_kscale(k):
    if not WIDE:
        return np.ones(k)
    levels = np.array([10, -10, 5, -5, 0])
    if k % 512:
        return np.exp2(np.random.permutation(np.resize(levels, k // 32))).repeat(32)
    a = np.empty((k // 512, 16))
    for p in range(k // 512):
        a[p, :8] = np.random.permutation(np.resize(levels, 8))
        for g in range(8):
            far = levels[np.abs(levels - a[p, g]) >= 10]
            a[p, g + 8] = far[np.random.randint(len(far))]
    return np.exp2(a.ravel()).repeat(32)


def f64(x):
    return np.asarray(x).astype(np.float64)


def striped(idx):
    return np.tile(idx.reshape(-1, 16).T, (8, 1)).astype(np.uint16)


def unstriped(offs):
    return offs[:16].T.reshape(-1).astype(np.int64)


def striped8(idx):
    return np.concatenate([x.reshape(-1, 16).T for x in idx]).astype(np.uint16)


def runs(offs, k):
    lists = np.stack([offs[16 * r : 16 * r + 16].T.reshape(-1) for r in range(8)]).astype(np.int64)
    return lists[np.arange(k) % 512 // 64]


def pack_weight(w):
    k, n = w.shape
    w = f64(np.asarray(w, np.float32).astype(ml_dtypes.bfloat16)).reshape(k // 32, 32, n)
    amax = np.abs(w).max(1)
    byte = np.clip(np.where(amax > 0, np.frexp(amax)[1] - 1 + 127 - 7, 1), 1, 254)
    scaled = (w * np.exp2(127.0 - byte)[:, None, :]).reshape(k, n).astype(np.float32)
    words = np.ascontiguousarray(scaled.reshape(k // 512, 128, 4, n).transpose(0, 1, 3, 2)).astype(ml_dtypes.float8_e4m3fn).view(np.uint8)
    return words, np.ascontiguousarray(byte.astype(np.uint8).reshape(k // 512, 16, n))


def unpack_weight(words, scales):
    g, p, n, _ = words.shape
    vals = np.ascontiguousarray(words).view(ml_dtypes.float8_e4m3fn).astype(np.float64) * np.repeat(np.exp2(scales.astype(np.float64) - 127.0), 8, axis=1)[..., None]
    return vals.transpose(0, 1, 3, 2).reshape(g * 512, n)


E2M1 = np.array([0.0, 0.5, 1.0, 1.5, 2.0, 3.0, 4.0, 6.0, -0.0, -0.5, -1.0, -1.5, -2.0, -3.0, -4.0, -6.0])


def pack_fp4(w):
    k, n = w.shape
    w = f64(np.asarray(w, np.float32).astype(ml_dtypes.bfloat16)).reshape(k // 32, 32, n)
    amax = np.abs(w).max(1)
    mant, ex = np.frexp(amax / 6.0)
    byte = np.clip(np.where(amax > 0, np.where(mant > 0.5, ex, ex - 1) + 127, 1), 1, 254)
    scaled = (w * np.exp2(127.0 - byte)[:, None, :]).reshape(k, n).astype(np.float32)
    c = np.ascontiguousarray(scaled.reshape(k // 512, 128, 4, n).transpose(0, 1, 3, 2)).astype(ml_dtypes.float4_e2m1fn).view(np.uint8) & 0xF
    words = (c[..., 0::2] | (c[..., 1::2] << 4)).reshape(k // 512, 128, 2 * n)
    return np.ascontiguousarray(words), np.ascontiguousarray(byte.astype(np.uint8).reshape(k // 512, 16, n))


def unpack_fp4(words, scales):
    g, _, n = scales.shape
    words = np.ascontiguousarray(words).reshape(g, 128, n, 2)
    nib = np.empty((g, 128, n, 4), np.uint8)
    nib[..., 0::2] = words & 0xF
    nib[..., 1::2] = words >> 4
    vals = E2M1[nib] * np.repeat(np.exp2(scales.astype(np.float64) - 127.0), 8, axis=1)[..., None]
    return vals.transpose(0, 1, 3, 2).reshape(g * 512, n)


def sigmoid(v):
    return 1.0 / (1.0 + np.exp(-np.maximum(v, -700.0)))


K, T, S, N, G, H, W, U = 512, 1024, 512, 512, 2048, 512, 256, 1024


def setup_inputs():
    n = np.random.standard_normal
    s = mx_kscale(K)[:, None]
    u = mx_kscale(S)
    packed_xT = pack_weight(n((K, T)) * s)
    packed_dT = pack_weight(n((K, G)) / s)
    packed_w1 = pack_fp4(n((H, N)) / np.sqrt(2 * H) / u[:, None])
    packed_w2 = pack_fp4(n((K, N)) / np.sqrt(2 * K) / s)
    perm = np.stack([np.random.permutation(S) for _ in range(8)])
    perm2 = np.random.permutation(U)
    return {
        "x_words": packed_xT[0],
        "x_scales": packed_xT[1],
        "d_words": packed_dT[0],
        "d_scales": packed_dT[1],
        "gn": (np.random.uniform(0.5, 1.5, (H, 1)) * u[:, None]).astype(np.float32),
        "w1_words": packed_w1[0],
        "w1_scales": packed_w1[1],
        "w2_words": packed_w2[0],
        "w2_scales": packed_w2[1],
        "sl": np.random.uniform(1.0, 2.0, (N, 1)).astype(np.float32),
        "th": (0.5 * n((N, 1))).astype(np.float32),
        "offs": striped8(np.random.randint(0, T, (8, S))),
        "ci": striped(np.random.permutation(G)[:H]),
        "n1": striped8(perm[:, :W]),
        "n2": striped8(perm[:, W:]),
        "two": striped(np.random.permutation(T)[:S]),
        "n3": striped(perm2[:S]),
        "n4": striped(perm2[S:]),
        "n5": striped(np.random.permutation(S)),
    }


def reference(x_words, x_scales, d_words, d_scales, gn, w1_words, w1_scales, w2_words, w2_scales, sl, th, offs, ci, n1, n2, two, n3, n4, n5):
    d_ci = unpack_weight(d_words, d_scales)[:, unstriped(ci)]
    xq = unpack_weight(x_words, x_scales)[np.arange(K)[:, None], runs(offs, K)]
    s = 0.0625 * (d_ci.T @ xq)
    pa = s[np.arange(H)[:, None], runs(n1, H)]
    pb = s[np.arange(H)[:, None], runs(n2, H)]
    ra = np.maximum(pa, pb)
    ds = s.copy()
    ds[np.arange(H)[:, None], runs(n1, H)] = ra
    z = f64(gn) * ds
    x_two = unpack_weight(x_words, x_scales)[:, unstriped(two)]
    h2 = unpack_fp4(w1_words, w1_scales).T @ mxq(z, 0, "e4m3") + unpack_fp4(w2_words, w2_scales).T @ x_two
    sg = sigmoid(f64(sl) * (h2[:, unstriped(n5)] - f64(th)))
    st = h2 * sg
    ph = np.zeros((N, U))
    ph[:, unstriped(n3)] = h2
    out = ph.copy()
    out[:, unstriped(n4)] = st
    return out

@@ -1,0 +1,164 @@
+from contextlib import ExitStack
+
+import concourse.mybir as mybir
+
+K, T, S, N, G, H, W, U = 512, 1024, 512, 512, 2048, 512, 256, 1024
+FLOPS = 3 * 2 * 512 * 512 * 512
+
+F32 = mybir.dt.float32
+BF16 = mybir.dt.bfloat16
+I32 = mybir.dt.int32
+U32 = mybir.dt.uint32
+U16 = mybir.dt.uint16
+U8 = mybir.dt.uint8
+FP8X4 = mybir.dt.float8_e4m3fn_x4
+FP4X4 = mybir.dt.float4_e2m1fn_x4
+ACT = mybir.ActivationFunctionType
+ALU = mybir.AluOpType
+
+P = 128
+PACK = 4
+CH = 256
+
+
+def load_scale_rows(queue, tile, scales):
+    rows = scales[0].bitcast(I32)
+    for q in range(4):
+        queue.dma_start(out=tile[32 * q : 32 * (q + 1), :].bitcast(I32),
+                        in_=rows[4 * q : 4 * (q + 1), :].unsqueeze(0).broadcast_to([8, 4, rows.shape[1]]))
+
+
+def place_scale_rows(queue, plane, picked):
+    for b in range(4):
+        queue.dma_start(out=plane[b:P:32, :].bitcast(I32), in_=picked[8 * b : P : 32, :].bitcast(I32))
+
+
+def tile_picked_xhzntfillepag_none_p_kernel(
+    tc, x_words, x_scales, d_words, d_scales, gn, w1_words, w1_scales, w2_words, w2_scales, sl, th,
+    offs, ci, n1, n2, two, n3, n4, n5, out,
+):
+    nc = tc.nc
+    with ExitStack() as ctx:
+        lists = ctx.enter_context(tc.tile_pool(name="lists", bufs=1))
+        keep = ctx.enter_context(tc.tile_pool(name="keep", bufs=1))
+        psum = ctx.enter_context(tc.psum_pool(name="psum", bufs=1))
+
+        def load_list(src, name):
+            tile = lists.tile([P, src.shape[1]], U16, name=name)
+            nc.sync.dma_start(tile[:], src)
+            return tile
+
+        def mx_tile(width, dtype, name):
+            return keep.tile([P, width], dtype, name=name, align_bytes=64)
+
+        x_s = mx_tile(T, U8, "x_s")
+        x_w = mx_tile(T, U32, "x_w")
+        d_s = mx_tile(G, U8, "d_s")
+        d_w = mx_tile(G, U32, "d_w")
+        offs_l = load_list(offs, "offs_l")
+        x_rows = x_scales[0].bitcast(I32)
+        nc.sync.dma_start(out=x_s[:].bitcast(I32), in_=x_rows.unsqueeze(1).broadcast_to([16, 8, T // 4]))
+        nc.sync.dma_start(out=x_w[:].bitcast(I32), in_=x_words[0].rearrange("p n t -> p (n t)").bitcast(I32))
+        ci_l = load_list(ci, "ci_l")
+        load_scale_rows(nc.sync, d_s, d_scales)
+        nc.sync.dma_start(out=d_w[:].bitcast(I32), in_=d_words[0].rearrange("p n t -> p (n t)").bitcast(I32))
+        two_l = load_list(two, "two_l")
+        n1_l = load_list(n1, "n1_l")
+
+        xq_b = mx_tile(S, U8, "xq_b")
+        xq_s = mx_tile(S, U8, "xq_s")
+        xq_w = mx_tile(S, U32, "xq_w")
+        dg_s = mx_tile(H, U8, "dg_s")
+        dg_w = mx_tile(H, U32, "dg_w")
+        x2_s = mx_tile(S, U8, "x2_s")
+        x2_w = mx_tile(S, U32, "x2_w")
+        x2_b = mx_tile(S, U8, "x2_b")
+        nc.gpsimd.memset(xq_s[:].bitcast(I32), 0)
+        nc.gpsimd.memset(x2_s[:].bitcast(I32), 0)
+
+        nc.vector.tensor_copy(xq_b[:], x_s[:].indirect(offs_l[:]))
+        place_scale_rows(nc.scalar, xq_s, xq_b)
+        nc.vector.tensor_copy(xq_w[:], x_w[:].indirect(offs_l[:]))
+        nc.vector.tensor_copy(dg_s[:].rearrange("p (t m) -> p m t", t=PACK), d_s[:].indirect(ci_l[:]))
+        nc.vector.tensor_copy(dg_w[:].rearrange("p (t m) -> p m t", t=PACK), d_w[:].indirect(ci_l[:]))
+        nc.vector.tensor_copy(x2_b[:], x_s[:].indirect(two_l[:]))
+        place_scale_rows(nc.sync, x2_s, x2_b)
+        nc.vector.tensor_copy(x2_w[:], x_w[:].indirect(two_l[:]))
+
+        n2_l = load_list(n2, "n2_l")
+        gain = keep.tile([P, PACK], F32, name="gain")
+        nc.sync.dma_start(out=gain[:], in_=gn.rearrange("(p t) o -> p (t o)", t=PACK))
+        w2_w = mx_tile(2 * N, U8, "w2_w")
+        w2_s = mx_tile(N, U8, "w2_s")
+        w1_w = mx_tile(2 * N, U8, "w1_w")
+        w1_s = mx_tile(N, U8, "w1_s")
+        nc.sync.dma_start(out=w2_w[:].bitcast(I32), in_=w2_words[0].bitcast(I32))
+        load_scale_rows(nc.sync, w2_s, w2_scales)
+        nc.sync.dma_start(out=w1_w[:].bitcast(I32), in_=w1_words[0].bitcast(I32))
+        load_scale_rows(nc.sync, w1_s, w1_scales)
+        n3_l = load_list(n3, "n3_l")
+        n5_l = load_list(n5, "n5_l")
+        n4_l = load_list(n4, "n4_l")
+        slope = keep.tile([P, N // P], F32, name="slope")
+        thresh = keep.tile([P, N // P], F32, name="thresh")
+        with nc.allow_non_contiguous_dma(reason="one value a row of h2"):
+            nc.sync.dma_start(out=slope[:], in_=sl.rearrange("(m p) o -> p (m o)", p=P))
+            nc.sync.dma_start(out=thresh[:], in_=th.rearrange("(m p) o -> p (m o)", p=P))
+        prod = keep.tile([P, N // P], F32, name="prod")
+        bias = keep.tile([P, N // P], F32, name="bias")
+        nc.gpsimd.tensor_tensor(prod[:], slope[:], thresh[:], ALU.mult)
+        nc.gpsimd.tensor_scalar(bias[:], prod[:], -1.0, 0.0, ALU.mult, ALU.add)
+
+        z_planes = keep.tile([P, PACK, S], BF16, name="z_planes", align_bytes=64)
+        rows = []
+        for t in range(PACK):
+            cols = slice(t * P, (t + 1) * P)
+            acc = psum.tile([P, S], F32, name=f"bank{t}")
+            nc.tensor.matmul_mx(out=acc[:], lhsT=dg_w[:, cols].bitcast(FP8X4), lhsT_scale=dg_s[:, cols],
+                                rhs=xq_w[:].bitcast(FP8X4), rhs_scale=xq_s[:], start=True, stop=True)
+            s_t = keep.tile([P, S], F32, name=f"s{t}")
+            pa = keep.tile([P, W], F32, name=f"pa{t}")
+            pb = keep.tile([P, W], F32, name=f"pb{t}")
+            ra = keep.tile([P, W], F32, name=f"ra{t}")
+            nc.scalar.activation(out=s_t[:], in_=acc[:], func=ACT.Copy, scale=0.0625)
+            nc.scalar.activation(out=pa[:], in_=s_t[:].indirect(n1_l[:]), func=ACT.Copy)
+            nc.scalar.activation(out=pb[:], in_=s_t[:].indirect(n2_l[:]), func=ACT.Copy)
+            nc.vector.tensor_tensor(ra[:], pa[:], pb[:], ALU.max)
+            nc.vector.tensor_copy(s_t[:].indirect(n1_l[:]), ra[:])
+            rows.append(s_t)
+        for t in range(PACK - 1):
+            nc.scalar.activation(out=z_planes[:, t, :], in_=rows[t][:], func=ACT.Copy, scale=gain[:, t : t + 1])
+        t = PACK - 1
+        nc.vector.tensor_scalar(z_planes[:, t, :], rows[t][:], gain[:, t : t + 1], None, ALU.mult)
+
+        z_w = mx_tile(S, U32, "z_w")
+        z_s = mx_tile(S, U8, "z_s")
+        for c in range(S // CH):
+            cols = slice(c * CH, (c + 1) * CH)
+            woven = keep.tile([P, CH, PACK], BF16, name=f"woven{c}", align_bytes=64)
+            nc.vector.tensor_copy(woven[:], z_planes[:, :, cols].rearrange("p t j -> p j t"))
+            nc.vector.quantize_mx(out=z_w[:, cols].bitcast(FP8X4), scales=z_s[:, cols], in_=woven[:].rearrange("p j t -> p (j t)"))
+
+        for m in range(N // P):
+            wcols = slice(2 * m * P, 2 * (m + 1) * P)
+            scols = slice(m * P, (m + 1) * P)
+            h2 = keep.tile([P, S], F32, name=f"h2_{m}")
+            sg = keep.tile([P, S], F32, name=f"sg{m}")
+            page = keep.tile([P, U], F32, name=f"page{m}")
+            width = CH if m == 0 else S
+            for c in range(S // width):
+                cols = slice(c * width, (c + 1) * width)
+                bank = c if m == 0 else PACK + m
+                acc = psum.tile([P, S], F32, name=f"bank{bank}")
+                nc.tensor.matmul_mx(out=acc[:, :width], lhsT=w2_w[:, wcols].bitcast(FP4X4), lhsT_scale=w2_s[:, scols],
+                                    rhs=x2_w[:, cols].bitcast(FP8X4), rhs_scale=x2_s[:, cols], start=True, stop=False)
+                nc.tensor.matmul_mx(out=acc[:, :width], lhsT=w1_w[:, wcols].bitcast(FP4X4), lhsT_scale=w1_s[:, scols],
+                                    rhs=z_w[:, cols].bitcast(FP8X4), rhs_scale=z_s[:, cols], start=False, stop=True)
+                nc.scalar.copy(out=h2[:, cols], in_=acc[:, :width])
+                nc.vector.tensor_copy(page[:].indirect(n3_l[:, c * width // 16 : (c + 1) * width // 16]), h2[:, cols])
+            for c in range(2):
+                cols = slice(c * W, (c + 1) * W)
+                nc.scalar.activation(out=sg[:, cols], in_=h2[:].indirect(n5_l[:, c * W // 16 : (c + 1) * W // 16]),
+                                     func=ACT.Sigmoid, scale=slope[:, m : m + 1], bias=bias[:, m : m + 1])
+            nc.vector.tensor_tensor(page[:].indirect(n4_l[:]), h2[:], sg[:], ALU.mult)
+            nc.sync.dma_start(out=out[m * P : (m + 1) * P, :], in_=page[:])

@@ -18,12 +18,12 @@ ALU = mybir.AluOpType
 
 P = 128
 PACK = 4
-CH = 256
+CHUNKS = ((0, 128), (128, 256), (256, 512))
 
 
-def load_scale_rows(queue, tile, scales):
+def load_scale_rows(queues, tile, scales):
     rows = scales[0].bitcast(I32)
-    for q in range(4):
+    for q, queue in enumerate(queues):
         queue.dma_start(out=tile[32 * q : 32 * (q + 1), :].bitcast(I32),
                         in_=rows[4 * q : 4 * (q + 1), :].unsqueeze(0).broadcast_to([8, 4, rows.shape[1]]))
 
@@ -48,8 +48,8 @@ def tile_picked_xhzntfillepag_none_p_kernel(
             nc.sync.dma_start(tile[:], src)
             return tile
 
-        def mx_tile(width, dtype, name):
-            return keep.tile([P, width], dtype, name=name, align_bytes=64)
+        def mx_tile(width, dtype, name, tag=None):
+            return keep.tile([P, width], dtype, name=name, tag=tag or name, align_bytes=64)
 
         x_s = mx_tile(T, U8, "x_s")
         x_w = mx_tile(T, U32, "x_w")
@@ -58,52 +58,52 @@ def tile_picked_xhzntfillepag_none_p_kernel(
         offs_l = load_list(offs, "offs_l")
         x_rows = x_scales[0].bitcast(I32)
         nc.sync.dma_start(out=x_s[:].bitcast(I32), in_=x_rows.unsqueeze(1).broadcast_to([16, 8, T // 4]))
-        nc.sync.dma_start(out=x_w[:].bitcast(I32), in_=x_words[0].rearrange("p n t -> p (n t)").bitcast(I32))
         ci_l = load_list(ci, "ci_l")
-        load_scale_rows(nc.sync, d_s, d_scales)
-        nc.sync.dma_start(out=d_w[:].bitcast(I32), in_=d_words[0].rearrange("p n t -> p (n t)").bitcast(I32))
+        load_scale_rows((nc.scalar, nc.sync, nc.sync, nc.sync), d_s, d_scales)
+        nc.scalar.dma_start(out=x_w[:].bitcast(I32), in_=x_words[0].rearrange("p n t -> p (n t)").bitcast(I32))
+        nc.scalar.dma_start(out=d_w[:].bitcast(I32), in_=d_words[0].rearrange("p n t -> p (n t)").bitcast(I32))
         two_l = load_list(two, "two_l")
         n1_l = load_list(n1, "n1_l")
+        n2_l = load_list(n2, "n2_l")
 
         xq_b = mx_tile(S, U8, "xq_b")
         xq_s = mx_tile(S, U8, "xq_s")
         xq_w = mx_tile(S, U32, "xq_w")
         dg_s = mx_tile(H, U8, "dg_s")
-        dg_w = mx_tile(H, U32, "dg_w")
         x2_s = mx_tile(S, U8, "x2_s")
-        x2_w = mx_tile(S, U32, "x2_w")
-        x2_b = mx_tile(S, U8, "x2_b")
-        nc.gpsimd.memset(xq_s[:].bitcast(I32), 0)
-        nc.gpsimd.memset(x2_s[:].bitcast(I32), 0)
+        nc.vector.memset(xq_s[:].bitcast(I32), 0)
+        nc.vector.memset(x2_s[:].bitcast(I32), 0)
 
         nc.vector.tensor_copy(xq_b[:], x_s[:].indirect(offs_l[:]))
         place_scale_rows(nc.scalar, xq_s, xq_b)
         nc.vector.tensor_copy(xq_w[:], x_w[:].indirect(offs_l[:]))
         nc.vector.tensor_copy(dg_s[:].rearrange("p (t m) -> p m t", t=PACK), d_s[:].indirect(ci_l[:]))
+        dg_w = mx_tile(H, U32, "dg_w", tag="d_s")
         nc.vector.tensor_copy(dg_w[:].rearrange("p (t m) -> p m t", t=PACK), d_w[:].indirect(ci_l[:]))
+        x2_w = mx_tile(S, U32, "x2_w", tag="d_w")
+        nc.vector.tensor_copy(x2_w[:], x_w[:].indirect(two_l[:]))
+        x2_b = mx_tile(S, U8, "x2_b", tag="x_w")
         nc.vector.tensor_copy(x2_b[:], x_s[:].indirect(two_l[:]))
         place_scale_rows(nc.sync, x2_s, x2_b)
-        nc.vector.tensor_copy(x2_w[:], x_w[:].indirect(two_l[:]))
 
-        n2_l = load_list(n2, "n2_l")
         gain = keep.tile([P, PACK], F32, name="gain")
-        nc.sync.dma_start(out=gain[:], in_=gn.rearrange("(p t) o -> p (t o)", t=PACK))
-        w2_w = mx_tile(2 * N, U8, "w2_w")
-        w2_s = mx_tile(N, U8, "w2_s")
-        w1_w = mx_tile(2 * N, U8, "w1_w")
-        w1_s = mx_tile(N, U8, "w1_s")
-        nc.sync.dma_start(out=w2_w[:].bitcast(I32), in_=w2_words[0].bitcast(I32))
-        load_scale_rows(nc.sync, w2_s, w2_scales)
-        nc.sync.dma_start(out=w1_w[:].bitcast(I32), in_=w1_words[0].bitcast(I32))
-        load_scale_rows(nc.sync, w1_s, w1_scales)
+        nc.gpsimd.dma_start(out=gain[:], in_=gn.rearrange("(p t) o -> p (t o)", t=PACK))
+        w_w = mx_tile(4 * N, U8, "w_w", tag="x_s")
+        w_s = mx_tile(2 * N, U8, "w_s", tag="xq_b")
+        w2_w, w1_w = w_w[:, : 2 * N], w_w[:, 2 * N :]
+        w2_s, w1_s = w_s[:, :N], w_s[:, N:]
+        nc.sync.dma_start(out=w2_w.bitcast(I32), in_=w2_words[0].bitcast(I32))
+        nc.sync.dma_start(out=w1_w.bitcast(I32), in_=w1_words[0].bitcast(I32))
+        load_scale_rows([nc.sync] * 4, w2_s, w2_scales)
+        load_scale_rows([nc.sync] * 4, w1_s, w1_scales)
         n3_l = load_list(n3, "n3_l")
         n5_l = load_list(n5, "n5_l")
         n4_l = load_list(n4, "n4_l")
         slope = keep.tile([P, N // P], F32, name="slope")
         thresh = keep.tile([P, N // P], F32, name="thresh")
         with nc.allow_non_contiguous_dma(reason="one value a row of h2"):
-            nc.sync.dma_start(out=slope[:], in_=sl.rearrange("(m p) o -> p (m o)", p=P))
-            nc.sync.dma_start(out=thresh[:], in_=th.rearrange("(m p) o -> p (m o)", p=P))
+            nc.gpsimd.dma_start(out=slope[:], in_=sl.rearrange("(m p) o -> p (m o)", p=P))
+            nc.gpsimd.dma_start(out=thresh[:], in_=th.rearrange("(m p) o -> p (m o)", p=P))
         prod = keep.tile([P, N // P], F32, name="prod")
         bias = keep.tile([P, N // P], F32, name="bias")
         nc.gpsimd.tensor_tensor(prod[:], slope[:], thresh[:], ALU.mult)
@@ -129,25 +129,30 @@ def tile_picked_xhzntfillepag_none_p_kernel(
         for t in range(PACK - 1):
             nc.scalar.activation(out=z_planes[:, t, :], in_=rows[t][:], func=ACT.Copy, scale=gain[:, t : t + 1])
         t = PACK - 1
-        nc.vector.tensor_scalar(z_planes[:, t, :], rows[t][:], gain[:, t : t + 1], None, ALU.mult)
+        nc.vector.tensor_scalar(z_planes[:, t, :W], rows[t][:, :W], gain[:, t : t + 1], None, ALU.mult)
+        nc.scalar.activation(out=z_planes[:, t, W:], in_=rows[t][:, W:], func=ACT.Copy, scale=gain[:, t : t + 1])
 
         z_w = mx_tile(S, U32, "z_w")
         z_s = mx_tile(S, U8, "z_s")
-        for c in range(S // CH):
-            cols = slice(c * CH, (c + 1) * CH)
-            woven = keep.tile([P, CH, PACK], BF16, name=f"woven{c}", align_bytes=64)
-            nc.vector.tensor_copy(woven[:], z_planes[:, :, cols].rearrange("p t j -> p j t"))
-            nc.vector.quantize_mx(out=z_w[:, cols].bitcast(FP8X4), scales=z_s[:, cols], in_=woven[:].rearrange("p j t -> p (j t)"))
+        for c, (lo, hi) in enumerate(CHUNKS):
+            woven = keep.tile([P, hi - lo, PACK], BF16, name=f"woven{c}", align_bytes=64)
+            for a in range(lo, hi, P):
+                dst = woven[:, a - lo : a - lo + P, :].rearrange("p (c i) t -> p c t i", i=4)
+                src = z_planes[:, :, a : a + P].rearrange("p t (c i) -> p c t i", i=4)
+                if lo < W:
+                    nc.vector.tensor_copy(dst, src)
+                else:
+                    nc.scalar.copy(out=dst, in_=src)
+            nc.vector.quantize_mx(out=z_w[:, lo:hi].bitcast(FP8X4), scales=z_s[:, lo:hi], in_=woven[:].rearrange("p j t -> p (j t)"))
 
-        for m in range(N // P):
+        def product_and_first_scatter(m):
             wcols = slice(2 * m * P, 2 * (m + 1) * P)
             scols = slice(m * P, (m + 1) * P)
             h2 = keep.tile([P, S], F32, name=f"h2_{m}")
-            sg = keep.tile([P, S], F32, name=f"sg{m}")
             page = keep.tile([P, U], F32, name=f"page{m}")
-            width = CH if m == 0 else S
-            for c in range(S // width):
-                cols = slice(c * width, (c + 1) * width)
+            for c, (lo, hi) in enumerate(CHUNKS if m == 0 else ((0, S),)):
+                cols = slice(lo, hi)
+                width = hi - lo
                 bank = c if m == 0 else PACK + m
                 acc = psum.tile([P, S], F32, name=f"bank{bank}")
                 nc.tensor.matmul_mx(out=acc[:, :width], lhsT=w2_w[:, wcols].bitcast(FP4X4), lhsT_scale=w2_s[:, scols],
@@ -155,10 +160,20 @@ def tile_picked_xhzntfillepag_none_p_kernel(
                 nc.tensor.matmul_mx(out=acc[:, :width], lhsT=w1_w[:, wcols].bitcast(FP4X4), lhsT_scale=w1_s[:, scols],
                                     rhs=z_w[:, cols].bitcast(FP8X4), rhs_scale=z_s[:, cols], start=False, stop=True)
                 nc.scalar.copy(out=h2[:, cols], in_=acc[:, :width])
-                nc.vector.tensor_copy(page[:].indirect(n3_l[:, c * width // 16 : (c + 1) * width // 16]), h2[:, cols])
+                nc.vector.tensor_copy(page[:].indirect(n3_l[:, lo // 16 : hi // 16]), h2[:, cols])
+            return h2, page
+
+        def gate_and_second_scatter(m, h2, page):
+            sg = keep.tile([P, S], F32, name=f"sg{m}")
             for c in range(2):
                 cols = slice(c * W, (c + 1) * W)
                 nc.scalar.activation(out=sg[:, cols], in_=h2[:].indirect(n5_l[:, c * W // 16 : (c + 1) * W // 16]),
                                      func=ACT.Sigmoid, scale=slope[:, m : m + 1], bias=bias[:, m : m + 1])
             nc.vector.tensor_tensor(page[:].indirect(n4_l[:]), h2[:], sg[:], ALU.mult)
             nc.sync.dma_start(out=out[m * P : (m + 1) * P, :], in_=page[:])
+
+        blocks = [product_and_first_scatter(0)]
+        for m in range(1, N // P):
+            blocks.append(product_and_first_scatter(m))
+            gate_and_second_scatter(m - 1, *blocks[m - 1])
+        gate_and_second_scatter(N // P - 1, *blocks[-1])

@@ -65,6 +65,9 @@ def tile_picked_xhzntfillepag_none_p_kernel(
         two_l = load_list(two, "two_l")
         n1_l = load_list(n1, "n1_l")
         n2_l = load_list(n2, "n2_l")
+        n3_l = load_list(n3, "n3_l")
+        n5_l = load_list(n5, "n5_l")
+        n4_l = load_list(n4, "n4_l")
 
         xq_b = mx_tile(S, U8, "xq_b")
         xq_s = mx_tile(S, U8, "xq_s")
@@ -86,28 +89,20 @@ def tile_picked_xhzntfillepag_none_p_kernel(
         nc.vector.tensor_copy(x2_b[:], x_s[:].indirect(two_l[:]))
         place_scale_rows(nc.sync, x2_s, x2_b)
 
-        gain = keep.tile([P, PACK], F32, name="gain")
-        nc.gpsimd.dma_start(out=gain[:], in_=gn.rearrange("(p t) o -> p (t o)", t=PACK))
-        w_w = mx_tile(4 * N, U8, "w_w", tag="x_s")
-        w_s = mx_tile(2 * N, U8, "w_s", tag="xq_b")
-        w2_w, w1_w = w_w[:, : 2 * N], w_w[:, 2 * N :]
-        w2_s, w1_s = w_s[:, :N], w_s[:, N:]
-        nc.sync.dma_start(out=w2_w.bitcast(I32), in_=w2_words[0].bitcast(I32))
-        nc.sync.dma_start(out=w1_w.bitcast(I32), in_=w1_words[0].bitcast(I32))
-        load_scale_rows([nc.sync] * 4, w2_s, w2_scales)
-        load_scale_rows([nc.sync] * 4, w1_s, w1_scales)
-        n3_l = load_list(n3, "n3_l")
-        n5_l = load_list(n5, "n5_l")
-        n4_l = load_list(n4, "n4_l")
-        slope = keep.tile([P, N // P], F32, name="slope")
-        thresh = keep.tile([P, N // P], F32, name="thresh")
+        per_row = mx_tile(24, F32, "per_row", tag="xq_b")
+        gain, slope, thresh = per_row[:, 0:4], per_row[:, 8:12], per_row[:, 16:20]
+        nc.sync.dma_start(out=gain, in_=gn.rearrange("(p t) o -> p (t o)", t=PACK))
         with nc.allow_non_contiguous_dma(reason="one value a row of h2"):
-            nc.gpsimd.dma_start(out=slope[:], in_=sl.rearrange("(m p) o -> p (m o)", p=P))
-            nc.gpsimd.dma_start(out=thresh[:], in_=th.rearrange("(m p) o -> p (m o)", p=P))
+            nc.sync.dma_start(out=slope, in_=sl.rearrange("(m p) o -> p (m o)", p=P))
+            nc.sync.dma_start(out=thresh, in_=th.rearrange("(m p) o -> p (m o)", p=P))
         prod = keep.tile([P, N // P], F32, name="prod")
         bias = keep.tile([P, N // P], F32, name="bias")
-        nc.gpsimd.tensor_tensor(prod[:], slope[:], thresh[:], ALU.mult)
+        nc.gpsimd.tensor_tensor(prod[:], slope, thresh, ALU.mult)
         nc.gpsimd.tensor_scalar(bias[:], prod[:], -1.0, 0.0, ALU.mult, ALU.add)
+        w_w = mx_tile(4 * N, U8, "w_w", tag="x_s")
+        w2_w, w1_w = w_w[:, : 2 * N], w_w[:, 2 * N :]
+        nc.sync.dma_start(out=w2_w.bitcast(I32), in_=w2_words[0].bitcast(I32))
+        nc.sync.dma_start(out=w1_w.bitcast(I32), in_=w1_words[0].bitcast(I32))
 
         z_planes = keep.tile([P, PACK, S], BF16, name="z_planes", align_bytes=64)
         rows = []
@@ -117,7 +112,7 @@ def tile_picked_xhzntfillepag_none_p_kernel(
             nc.tensor.matmul_mx(out=acc[:], lhsT=dg_w[:, cols].bitcast(FP8X4), lhsT_scale=dg_s[:, cols],
                                 rhs=xq_w[:].bitcast(FP8X4), rhs_scale=xq_s[:], start=True, stop=True)
             s_t = keep.tile([P, S], F32, name=f"s{t}")
-            pa = keep.tile([P, W], F32, name=f"pa{t}")
+            pa = mx_tile(W, F32, f"pa{t}")
             pb = keep.tile([P, W], F32, name=f"pb{t}")
             ra = keep.tile([P, W], F32, name=f"ra{t}")
             nc.scalar.activation(out=s_t[:], in_=acc[:], func=ACT.Copy, scale=0.0625)
@@ -126,6 +121,10 @@ def tile_picked_xhzntfillepag_none_p_kernel(
             nc.vector.tensor_tensor(ra[:], pa[:], pb[:], ALU.max)
             nc.vector.tensor_copy(s_t[:].indirect(n1_l[:]), ra[:])
             rows.append(s_t)
+        w_s = mx_tile(2 * N, U8, "w_s", tag="pa0")
+        w2_s, w1_s = w_s[:, :N], w_s[:, N:]
+        load_scale_rows([nc.sync] * 4, w2_s, w2_scales)
+        load_scale_rows([nc.sync] * 4, w1_s, w1_scales)
         for t in range(PACK - 1):
             nc.scalar.activation(out=z_planes[:, t, :], in_=rows[t][:], func=ACT.Copy, scale=gain[:, t : t + 1])
         t = PACK - 1

@@ -21,13 +21,6 @@ PACK = 4
 CHUNKS = ((0, 128), (128, 256), (256, 512))
 
 
-def load_scale_rows(queues, tile, scales):
-    rows = scales[0].bitcast(I32)
-    for q, queue in enumerate(queues):
-        queue.dma_start(out=tile[32 * q : 32 * (q + 1), :].bitcast(I32),
-                        in_=rows[4 * q : 4 * (q + 1), :].unsqueeze(0).broadcast_to([8, 4, rows.shape[1]]))
-
-
 def place_scale_rows(queue, plane, picked):
     for b in range(4):
         queue.dma_start(out=plane[b:P:32, :].bitcast(I32), in_=picked[8 * b : P : 32, :].bitcast(I32))
@@ -51,6 +44,12 @@ def tile_picked_xhzntfillepag_none_p_kernel(
         def mx_tile(width, dtype, name, tag=None):
             return keep.tile([P, width], dtype, name=name, tag=tag or name, align_bytes=64)
 
+        def load_scale_rows(tile, scales):
+            rows = scales[0].bitcast(I32)
+            for q in range(4):
+                nc.sync.dma_start(out=tile[32 * q : 32 * (q + 1), :].bitcast(I32),
+                                  in_=rows[4 * q : 4 * (q + 1), :].unsqueeze(0).broadcast_to([8, 4, rows.shape[1]]))
+
         x_s = mx_tile(T, U8, "x_s")
         x_w = mx_tile(T, U32, "x_w")
         d_s = mx_tile(G, U8, "d_s")
@@ -58,11 +57,11 @@ def tile_picked_xhzntfillepag_none_p_kernel(
         offs_l = load_list(offs, "offs_l")
         x_rows = x_scales[0].bitcast(I32)
         nc.sync.dma_start(out=x_s[:].bitcast(I32), in_=x_rows.unsqueeze(1).broadcast_to([16, 8, T // 4]))
-        ci_l = load_list(ci, "ci_l")
-        load_scale_rows((nc.scalar, nc.sync, nc.sync, nc.sync), d_s, d_scales)
-        nc.scalar.dma_start(out=x_w[:].bitcast(I32), in_=x_words[0].rearrange("p n t -> p (n t)").bitcast(I32))
-        nc.scalar.dma_start(out=d_w[:].bitcast(I32), in_=d_words[0].rearrange("p n t -> p (n t)").bitcast(I32))
+        nc.sync.dma_start(out=x_w[:].bitcast(I32), in_=x_words[0].rearrange("p n t -> p (n t)").bitcast(I32))
         two_l = load_list(two, "two_l")
+        ci_l = load_list(ci, "ci_l")
+        load_scale_rows(d_s, d_scales)
+        nc.sync.dma_start(out=d_w[:].bitcast(I32), in_=d_words[0].rearrange("p n t -> p (n t)").bitcast(I32))
         n1_l = load_list(n1, "n1_l")
         n2_l = load_list(n2, "n2_l")
         n3_l = load_list(n3, "n3_l")
@@ -80,12 +79,12 @@ def tile_picked_xhzntfillepag_none_p_kernel(
         nc.vector.tensor_copy(xq_b[:], x_s[:].indirect(offs_l[:]))
         place_scale_rows(nc.scalar, xq_s, xq_b)
         nc.vector.tensor_copy(xq_w[:], x_w[:].indirect(offs_l[:]))
-        nc.vector.tensor_copy(dg_s[:].rearrange("p (t m) -> p m t", t=PACK), d_s[:].indirect(ci_l[:]))
-        dg_w = mx_tile(H, U32, "dg_w", tag="d_s")
-        nc.vector.tensor_copy(dg_w[:].rearrange("p (t m) -> p m t", t=PACK), d_w[:].indirect(ci_l[:]))
-        x2_w = mx_tile(S, U32, "x2_w", tag="d_w")
+        x2_w = mx_tile(S, U32, "x2_w")
         nc.vector.tensor_copy(x2_w[:], x_w[:].indirect(two_l[:]))
-        x2_b = mx_tile(S, U8, "x2_b", tag="x_w")
+        nc.vector.tensor_copy(dg_s[:].rearrange("p (t m) -> p m t", t=PACK), d_s[:].indirect(ci_l[:]))
+        dg_w = mx_tile(H, U32, "dg_w")
+        nc.vector.tensor_copy(dg_w[:].rearrange("p (t m) -> p m t", t=PACK), d_w[:].indirect(ci_l[:]))
+        x2_b = mx_tile(S, U8, "x2_b", tag="d_w")
         nc.vector.tensor_copy(x2_b[:], x_s[:].indirect(two_l[:]))
         place_scale_rows(nc.sync, x2_s, x2_b)
 
@@ -104,27 +103,31 @@ def tile_picked_xhzntfillepag_none_p_kernel(
         nc.sync.dma_start(out=w2_w.bitcast(I32), in_=w2_words[0].bitcast(I32))
         nc.sync.dma_start(out=w1_w.bitcast(I32), in_=w1_words[0].bitcast(I32))
 
-        z_planes = keep.tile([P, PACK, S], BF16, name="z_planes", align_bytes=64)
+        w_s = mx_tile(2 * N, U8, "w_s", tag="x_w")
+        w2_s, w1_s = w_s[:, :N], w_s[:, N:]
+        load_scale_rows(w2_s, w2_scales)
+        load_scale_rows(w1_s, w1_scales)
+
         rows = []
         for t in range(PACK):
             cols = slice(t * P, (t + 1) * P)
-            acc = psum.tile([P, S], F32, name=f"bank{t}")
+            acc = psum.tile([P, S], F32, name="score_bank")
             nc.tensor.matmul_mx(out=acc[:], lhsT=dg_w[:, cols].bitcast(FP8X4), lhsT_scale=dg_s[:, cols],
                                 rhs=xq_w[:].bitcast(FP8X4), rhs_scale=xq_s[:], start=True, stop=True)
             s_t = keep.tile([P, S], F32, name=f"s{t}")
             pa = mx_tile(W, F32, f"pa{t}")
-            pb = keep.tile([P, W], F32, name=f"pb{t}")
+            pb = mx_tile(W, F32, f"pb{t}")
             ra = keep.tile([P, W], F32, name=f"ra{t}")
             nc.scalar.activation(out=s_t[:], in_=acc[:], func=ACT.Copy, scale=0.0625)
-            nc.scalar.activation(out=pa[:], in_=s_t[:].indirect(n1_l[:]), func=ACT.Copy)
+            if t == 0:
+                nc.vector.tensor_copy(pa[:], s_t[:].indirect(n1_l[:]))
+            else:
+                nc.scalar.activation(out=pa[:], in_=s_t[:].indirect(n1_l[:]), func=ACT.Copy)
             nc.scalar.activation(out=pb[:], in_=s_t[:].indirect(n2_l[:]), func=ACT.Copy)
             nc.vector.tensor_tensor(ra[:], pa[:], pb[:], ALU.max)
             nc.vector.tensor_copy(s_t[:].indirect(n1_l[:]), ra[:])
             rows.append(s_t)
-        w_s = mx_tile(2 * N, U8, "w_s", tag="pa0")
-        w2_s, w1_s = w_s[:, :N], w_s[:, N:]
-        load_scale_rows([nc.sync] * 4, w2_s, w2_scales)
-        load_scale_rows([nc.sync] * 4, w1_s, w1_scales)
+        z_planes = keep.tile([P, PACK, S], BF16, name="z_planes", tag="pb2", align_bytes=64)
         for t in range(PACK - 1):
             nc.scalar.activation(out=z_planes[:, t, :], in_=rows[t][:], func=ACT.Copy, scale=gain[:, t : t + 1])
         t = PACK - 1
@@ -136,8 +139,8 @@ def tile_picked_xhzntfillepag_none_p_kernel(
         for c, (lo, hi) in enumerate(CHUNKS):
             woven = keep.tile([P, hi - lo, PACK], BF16, name=f"woven{c}", align_bytes=64)
             for a in range(lo, hi, P):
-                dst = woven[:, a - lo : a - lo + P, :].rearrange("p (c i) t -> p c t i", i=4)
-                src = z_planes[:, :, a : a + P].rearrange("p t (c i) -> p c t i", i=4)
+                dst = woven[:, a - lo : a - lo + P, :]
+                src = z_planes[:, :, a : a + P].rearrange("p t j -> p j t")
                 if lo < W:
                     nc.vector.tensor_copy(dst, src)
                 else:

from contextlib import ExitStack

import concourse.mybir as mybir

K, T, S, N, G, H, W, U = 512, 1024, 512, 512, 2048, 512, 256, 1024
FLOPS = 3 * 2 * 512 * 512 * 512

F32 = mybir.dt.float32
BF16 = mybir.dt.bfloat16
I32 = mybir.dt.int32
U32 = mybir.dt.uint32
U16 = mybir.dt.uint16
U8 = mybir.dt.uint8
FP8X4 = mybir.dt.float8_e4m3fn_x4
FP4X4 = mybir.dt.float4_e2m1fn_x4
ACT = mybir.ActivationFunctionType
ALU = mybir.AluOpType

P = 128
PACK = 4
CHUNKS = ((0, 128), (128, 256), (256, 512))


def place_scale_rows(queue, plane, picked):
    for b in range(4):
        queue.dma_start(out=plane[b:P:32, :].bitcast(I32), in_=picked[8 * b : P : 32, :].bitcast(I32))


def tile_picked_xhzntfillepag_none_p_kernel(
    tc, x_words, x_scales, d_words, d_scales, gn, w1_words, w1_scales, w2_words, w2_scales, sl, th,
    offs, ci, n1, n2, two, n3, n4, n5, out,
):
    nc = tc.nc
    with ExitStack() as ctx:
        lists = ctx.enter_context(tc.tile_pool(name="lists", bufs=1))
        keep = ctx.enter_context(tc.tile_pool(name="keep", bufs=1))
        psum = ctx.enter_context(tc.psum_pool(name="psum", bufs=1))

        def load_list(src, name):
            tile = lists.tile([P, src.shape[1]], U16, name=name)
            nc.sync.dma_start(tile[:], src)
            return tile

        def mx_tile(width, dtype, name, tag=None):
            return keep.tile([P, width], dtype, name=name, tag=tag or name, align_bytes=64)

        def load_scale_rows(tile, scales):
            rows = scales[0].bitcast(I32)
            for q in range(4):
                nc.sync.dma_start(out=tile[32 * q : 32 * (q + 1), :].bitcast(I32),
                                  in_=rows[4 * q : 4 * (q + 1), :].unsqueeze(0).broadcast_to([8, 4, rows.shape[1]]))

        x_s = mx_tile(T, U8, "x_s")
        x_w = mx_tile(T, U32, "x_w")
        d_s = mx_tile(G, U8, "d_s")
        d_w = mx_tile(G, U32, "d_w")
        offs_l = load_list(offs, "offs_l")
        x_rows = x_scales[0].bitcast(I32)
        nc.sync.dma_start(out=x_s[:].bitcast(I32), in_=x_rows.unsqueeze(1).broadcast_to([16, 8, T // 4]))
        nc.sync.dma_start(out=x_w[:].bitcast(I32), in_=x_words[0].rearrange("p n t -> p (n t)").bitcast(I32))
        two_l = load_list(two, "two_l")
        ci_l = load_list(ci, "ci_l")
        load_scale_rows(d_s, d_scales)
        nc.sync.dma_start(out=d_w[:].bitcast(I32), in_=d_words[0].rearrange("p n t -> p (n t)").bitcast(I32))
        n1_l = load_list(n1, "n1_l")
        n2_l = load_list(n2, "n2_l")
        n3_l = load_list(n3, "n3_l")
        n5_l = load_list(n5, "n5_l")
        n4_l = load_list(n4, "n4_l")

        xq_b = mx_tile(S, U8, "xq_b")
        xq_s = mx_tile(S, U8, "xq_s")
        xq_w = mx_tile(S, U32, "xq_w")
        dg_s = mx_tile(H, U8, "dg_s")
        x2_s = mx_tile(S, U8, "x2_s")
        nc.vector.memset(xq_s[:].bitcast(I32), 0)
        nc.vector.memset(x2_s[:].bitcast(I32), 0)

        nc.vector.tensor_copy(xq_b[:], x_s[:].indirect(offs_l[:]))
        place_scale_rows(nc.scalar, xq_s, xq_b)
        nc.vector.tensor_copy(xq_w[:], x_w[:].indirect(offs_l[:]))
        x2_w = mx_tile(S, U32, "x2_w")
        nc.vector.tensor_copy(x2_w[:], x_w[:].indirect(two_l[:]))
        nc.vector.tensor_copy(dg_s[:].rearrange("p (t m) -> p m t", t=PACK), d_s[:].indirect(ci_l[:]))
        dg_w = mx_tile(H, U32, "dg_w")
        nc.vector.tensor_copy(dg_w[:].rearrange("p (t m) -> p m t", t=PACK), d_w[:].indirect(ci_l[:]))
        x2_b = mx_tile(S, U8, "x2_b", tag="d_w")
        nc.vector.tensor_copy(x2_b[:], x_s[:].indirect(two_l[:]))
        place_scale_rows(nc.sync, x2_s, x2_b)

        per_row = mx_tile(24, F32, "per_row", tag="xq_b")
        gain, slope, thresh = per_row[:, 0:4], per_row[:, 8:12], per_row[:, 16:20]
        nc.sync.dma_start(out=gain, in_=gn.rearrange("(p t) o -> p (t o)", t=PACK))
        with nc.allow_non_contiguous_dma(reason="one value a row of h2"):
            nc.sync.dma_start(out=slope, in_=sl.rearrange("(m p) o -> p (m o)", p=P))
            nc.sync.dma_start(out=thresh, in_=th.rearrange("(m p) o -> p (m o)", p=P))
        prod = keep.tile([P, N // P], F32, name="prod")
        bias = keep.tile([P, N // P], F32, name="bias")
        nc.gpsimd.tensor_tensor(prod[:], slope, thresh, ALU.mult)
        nc.gpsimd.tensor_scalar(bias[:], prod[:], -1.0, 0.0, ALU.mult, ALU.add)
        w_w = mx_tile(4 * N, U8, "w_w", tag="x_s")
        w2_w, w1_w = w_w[:, : 2 * N], w_w[:, 2 * N :]
        nc.sync.dma_start(out=w2_w.bitcast(I32), in_=w2_words[0].bitcast(I32))
        nc.sync.dma_start(out=w1_w.bitcast(I32), in_=w1_words[0].bitcast(I32))

        w_s = mx_tile(2 * N, U8, "w_s", tag="x_w")
        w2_s, w1_s = w_s[:, :N], w_s[:, N:]
        load_scale_rows(w2_s, w2_scales)
        load_scale_rows(w1_s, w1_scales)

        rows = []
        for t in range(PACK):
            cols = slice(t * P, (t + 1) * P)
            acc = psum.tile([P, S], F32, name="score_bank")
            nc.tensor.matmul_mx(out=acc[:], lhsT=dg_w[:, cols].bitcast(FP8X4), lhsT_scale=dg_s[:, cols],
                                rhs=xq_w[:].bitcast(FP8X4), rhs_scale=xq_s[:], start=True, stop=True)
            s_t = keep.tile([P, S], F32, name=f"s{t}")
            pa = mx_tile(W, F32, f"pa{t}")
            pb = mx_tile(W, F32, f"pb{t}")
            ra = keep.tile([P, W], F32, name=f"ra{t}")
            nc.scalar.activation(out=s_t[:], in_=acc[:], func=ACT.Copy, scale=0.0625)
            if t == 0:
                nc.vector.tensor_copy(pa[:], s_t[:].indirect(n1_l[:]))
            else:
                nc.scalar.activation(out=pa[:], in_=s_t[:].indirect(n1_l[:]), func=ACT.Copy)
            nc.scalar.activation(out=pb[:], in_=s_t[:].indirect(n2_l[:]), func=ACT.Copy)
            nc.vector.tensor_tensor(ra[:], pa[:], pb[:], ALU.max)
            nc.vector.tensor_copy(s_t[:].indirect(n1_l[:]), ra[:])
            rows.append(s_t)
        z_planes = keep.tile([P, PACK, S], BF16, name="z_planes", tag="pb2", align_bytes=64)
        for t in range(PACK - 1):
            nc.scalar.activation(out=z_planes[:, t, :], in_=rows[t][:], func=ACT.Copy, scale=gain[:, t : t + 1])
        t = PACK - 1
        nc.vector.tensor_scalar(z_planes[:, t, :W], rows[t][:, :W], gain[:, t : t + 1], None, ALU.mult)
        nc.scalar.activation(out=z_planes[:, t, W:], in_=rows[t][:, W:], func=ACT.Copy, scale=gain[:, t : t + 1])

        z_w = mx_tile(S, U32, "z_w")
        z_s = mx_tile(S, U8, "z_s")
        for c, (lo, hi) in enumerate(CHUNKS):
            woven = keep.tile([P, hi - lo, PACK], BF16, name=f"woven{c}", align_bytes=64)
            for a in range(lo, hi, P):
                dst = woven[:, a - lo : a - lo + P, :]
                src = z_planes[:, :, a : a + P].rearrange("p t j -> p j t")
                if lo < W:
                    nc.vector.tensor_copy(dst, src)
                else:
                    nc.scalar.copy(out=dst, in_=src)
            nc.vector.quantize_mx(out=z_w[:, lo:hi].bitcast(FP8X4), scales=z_s[:, lo:hi], in_=woven[:].rearrange("p j t -> p (j t)"))

        def product_and_first_scatter(m):
            wcols = slice(2 * m * P, 2 * (m + 1) * P)
            scols = slice(m * P, (m + 1) * P)
            h2 = keep.tile([P, S], F32, name=f"h2_{m}")
            page = keep.tile([P, U], F32, name=f"page{m}")
            for c, (lo, hi) in enumerate(CHUNKS if m == 0 else ((0, S),)):
                cols = slice(lo, hi)
                width = hi - lo
                bank = c if m == 0 else PACK + m
                acc = psum.tile([P, S], F32, name=f"bank{bank}")
                nc.tensor.matmul_mx(out=acc[:, :width], lhsT=w2_w[:, wcols].bitcast(FP4X4), lhsT_scale=w2_s[:, scols],
                                    rhs=x2_w[:, cols].bitcast(FP8X4), rhs_scale=x2_s[:, cols], start=True, stop=False)
                nc.tensor.matmul_mx(out=acc[:, :width], lhsT=w1_w[:, wcols].bitcast(FP4X4), lhsT_scale=w1_s[:, scols],
                                    rhs=z_w[:, cols].bitcast(FP8X4), rhs_scale=z_s[:, cols], start=False, stop=True)
                nc.scalar.copy(out=h2[:, cols], in_=acc[:, :width])
                nc.vector.tensor_copy(page[:].indirect(n3_l[:, lo // 16 : hi // 16]), h2[:, cols])
            return h2, page

        def gate_and_second_scatter(m, h2, page):
            sg = keep.tile([P, S], F32, name=f"sg{m}")
            for c in range(2):
                cols = slice(c * W, (c + 1) * W)
                nc.scalar.activation(out=sg[:, cols], in_=h2[:].indirect(n5_l[:, c * W // 16 : (c + 1) * W // 16]),
                                     func=ACT.Sigmoid, scale=slope[:, m : m + 1], bias=bias[:, m : m + 1])
            nc.vector.tensor_tensor(page[:].indirect(n4_l[:]), h2[:], sg[:], ALU.mult)
            nc.sync.dma_start(out=out[m * P : (m + 1) * P, :], in_=page[:])

        blocks = [product_and_first_scatter(0)]
        for m in range(1, N // P):
            blocks.append(product_and_first_scatter(m))
            gate_and_second_scatter(m - 1, *blocks[m - 1])
        gate_and_second_scatter(N // P - 1, *blocks[-1])
